import numpy as np
import ml_dtypes


def mxq(x, axis, fmt="e4m3"):
    dtype, down = {"e4m3": (ml_dtypes.float8_e4m3fn, 7), "e5m2": (ml_dtypes.float8_e5m2, 14)}[fmt]
    v = np.moveaxis(np.asarray(x, np.float32).astype(ml_dtypes.bfloat16).astype(np.float64), axis, -1)
    blocks = v.reshape(v.shape[:-1] + (-1, 32))
    amax = np.abs(blocks).max(-1, keepdims=True)
    byte = np.maximum(np.where(amax > 0, np.frexp(amax)[1] - 1 + 127, 0) - down, 1)
    scale = np.exp2(byte - 127.0)
    codes = (blocks / scale).astype(np.float32).astype(dtype).astype(np.float64)
    return np.moveaxis((codes * scale).reshape(v.shape), -1, axis)


WIDE = False


def mx_kscale(k):
    if not WIDE:
        return np.ones(k)
    levels = np.array([10, -10, 5, -5, 0])
    if k % 512:
        return np.exp2(np.random.permutation(np.resize(levels, k // 32))).repeat(32)
    a = np.empty((k // 512, 16))
    for p in range(k // 512):
        a[p, :8] = np.random.permutation(np.resize(levels, 8))
        for g in range(8):
            far = levels[np.abs(levels - a[p, g]) >= 10]
            a[p, g + 8] = far[np.random.randint(len(far))]
    return np.exp2(a.ravel()).repeat(32)


def f64(x):
    return np.asarray(x).astype(np.float64)


def striped(idx):
    return np.tile(idx.reshape(-1, 16).T, (8, 1)).astype(np.uint16)


def unstriped(offs):
    return offs[:16].T.reshape(-1).astype(np.int64)


def pack_weight(w):
    k, n = w.shape
    w = f64(np.asarray(w, np.float32).astype(ml_dtypes.bfloat16)).reshape(k // 32, 32, n)
    amax = np.abs(w).max(1)
    byte = np.clip(np.where(amax > 0, np.frexp(amax)[1] - 1 + 127 - 7, 1), 1, 254)
    scaled = (w * np.exp2(127.0 - byte)[:, None, :]).reshape(k, n).astype(np.float32)
    words = np.ascontiguousarray(scaled.reshape(k // 512, 128, 4, n).transpose(0, 1, 3, 2)).astype(ml_dtypes.float8_e4m3fn).view(np.uint8)
    return words, np.ascontiguousarray(byte.astype(np.uint8).reshape(k // 512, 16, n))


def unpack_weight(words, scales):
    g, p, n, _ = words.shape
    vals = np.ascontiguousarray(words).view(ml_dtypes.float8_e4m3fn).astype(np.float64) * np.repeat(np.exp2(scales.astype(np.float64) - 127.0), 8, axis=1)[..., None]
    return vals.transpose(0, 1, 3, 2).reshape(g * 512, n)


K, T, S, D, N = 1024, 1024, 512, 4, 256
P = 2 ** 7


def setup_inputs():
    n = np.random.standard_normal
    s = mx_kscale(K)[:, None]
    packed_xT = pack_weight(n((K, T)) * s)
    return {
        "x_words": packed_xT[0],
        "x_scales": packed_xT[1],
        "w1": (n((K, N)) / np.sqrt(K) / s).astype(np.float32),
        "w2": (n((K, N)) / np.sqrt(K) / s).astype(np.float32),
        "strg": (np.tile(np.random.uniform(0.8, 1.6, S), (P, 1))).astype(np.float32),
        "offs": striped(np.random.permutation(T)[:S]),
        "rev": striped(np.random.permutation(S)),
    }


def reference(x_words, x_scales, w1, w2, strg, offs, rev):
    xq = unpack_weight(x_words, x_scales)[:, unstriped(offs)]
    y = mxq(f64(w1), 0, "e4m3").T @ xq
    rep = np.exp(-0.8 * y)
    z = mxq(f64(w2), 0, "e4m3").T @ xq
    ang = np.log(np.exp(z) + 1.0)
    gs = ang.reshape(len(ang), -1, D).sum(axis=2)
    zeta = np.repeat(gs, D, axis=1) - ang
    bo = f64(strg)[:1] / np.sqrt(0.8 * zeta + 1.0)
    attr = np.exp(-0.4 * y)
    return rep - ((0.5 * (bo + bo[:, unstriped(rev)])) * attr)

@@ -1,0 +1,199 @@
+from contextlib import ExitStack
+
+import concourse.mybir as mybir
+
+K, T, S, D, N = 1024, 1024, 512, 4, 256
+FLOPS = 2 * 2 * K * N * S
+
+F32 = mybir.dt.float32
+BF16 = mybir.dt.bfloat16
+I32 = mybir.dt.int32
+U32 = mybir.dt.uint32
+U16 = mybir.dt.uint16
+U8 = mybir.dt.uint8
+FP8X4 = mybir.dt.float8_e4m3fn_x4
+ALU = mybir.AluOpType
+ACT = mybir.ActivationFunctionType
+
+P = 128
+PACK = 4
+K_PASS = P * PACK
+PASSES = K // K_PASS
+TILES = N // P
+HALF = S // 2
+SOFTPLUS_LINEAR = 40.0
+
+
+def tile_picked_yterso_sym_p_kernel(tc, x_words, x_scales, w1, w2, strg, offs, rev, out):
+    nc = tc.nc
+    with ExitStack() as ctx:
+        keep = ctx.enter_context(tc.tile_pool(name="keep", bufs=1))
+        psum = ctx.enter_context(tc.psum_pool(name="psum", bufs=1))
+
+        def sb(shape, dtype, name):
+            return keep.tile(shape, dtype, name=name, align_bytes=64)
+
+        offs_t = keep.tile([P, S // 16], U16, name="offs_t")
+        rev_t = keep.tile([P, S // 16], U16, name="rev_t")
+        words = [sb([P, T], I32, f"words{o}") for o in range(PASSES)]
+        planes = sb([P, T], U8, "planes")
+        raw = {(w, o): sb([P, PACK, N], F32, f"raw{w}{o}") for w in (1, 2) for o in range(PASSES)}
+        strg_t = sb([P, S], F32, "strg_t")
+        weights = {1: w1, 2: w2}
+
+        def load_words(o):
+            nc.sync.dma_start(out=words[o][:], in_=x_words[o].rearrange("p n t -> p (n t)").bitcast(I32))
+
+        def load_weight(w, o):
+            rows = weights[w][o * K_PASS : (o + 1) * K_PASS, :]
+            nc.sync.dma_start(out=raw[w, o][:], in_=rows.rearrange("(p j) m -> p j m", j=PACK))
+
+        nc.vector.memset(planes[:].bitcast(I32), 0)
+        nc.sync.dma_start(offs_t[:], offs)
+        for q in range(4):
+            nc.sync.dma_start(
+                out=planes[32 * q : 32 * q + 4 * PASSES, :].bitcast(I32),
+                in_=x_scales[:, 4 * q : 4 * q + 4, :].bitcast(I32),
+            )
+        load_words(0)
+        load_weight(2, 0)
+        load_weight(2, 1)
+        load_words(1)
+        load_weight(1, 0)
+        load_weight(1, 1)
+        nc.sync.dma_start(rev_t[:], rev)
+        nc.sync.dma_start(out=strg_t[:], in_=strg)
+
+        picked = [sb([P, S], U32, f"picked{o}") for o in range(PASSES)]
+        picked_planes = sb([P, S], U8, "picked_planes")
+        grouped = {key: sb([P, N * PACK], BF16, f"grouped{key[0]}{key[1]}") for key in raw}
+        codes = {key: sb([P, N], U32, f"codes{key[0]}{key[1]}") for key in raw}
+        scales = {key: sb([P, N], U8, f"scales{key[0]}{key[1]}") for key in raw}
+
+        halves = [slice(c * HALF, (c + 1) * HALF) for c in range(2)]
+        list_halves = [slice(c * HALF // 16, (c + 1) * HALF // 16) for c in range(2)]
+
+        def views(key, lo, hi):
+            dst = grouped[key][:, lo * PACK : hi * PACK].rearrange("p (c i t) -> p c t i", i=4, t=PACK)
+            src = raw[key][:, :, lo:hi].rearrange("p t (c i) -> p c t i", i=4)
+            return dst, src
+
+        def interleave_scalar(key, lo=0, hi=N):
+            dst, src = views(key, lo, hi)
+            nc.scalar.activation(dst, src, ACT.Copy)
+
+        def interleave_vector(key, lo=0, hi=N):
+            dst, src = views(key, lo, hi)
+            nc.vector.tensor_copy(dst, src)
+
+        def quantise(key, lo=0, hi=N):
+            nc.vector.quantize_mx(
+                out=codes[key][:, lo:hi].bitcast(FP8X4),
+                scales=scales[key][:, lo:hi],
+                in_=grouped[key][:, lo * PACK : hi * PACK],
+            )
+
+        acc_z = {(h, c): psum.tile([P, HALF], F32, name=f"acc_z{h}{c}") for h in range(TILES) for c in range(2)}
+        acc_y = [psum.tile([P, S], F32, name=f"acc_y{h}") for h in range(TILES)]
+
+        def product(acc, w, o, h, cols):
+            rows = slice(h * P, (h + 1) * P)
+            nc.tensor.matmul_mx(
+                out=acc[:],
+                lhsT=codes[w, o][:, rows].bitcast(FP8X4),
+                lhsT_scale=scales[w, o][:, rows],
+                rhs=picked[o][:, cols].bitcast(FP8X4),
+                rhs_scale=picked_planes[4 * o : P, cols],
+                start=(o == 0),
+                stop=(o == PASSES - 1),
+            )
+
+        nc.vector.tensor_copy(picked_planes[:], planes[:].indirect(offs_t[:]))
+        nc.vector.tensor_copy(picked[0][:], words[0][:].bitcast(U32).indirect(offs_t[:]))
+        interleave_scalar((2, 0))
+        quantise((2, 0))
+        for c in range(2):
+            for h in range(TILES):
+                product(acc_z[h, c], 2, 0, h, halves[c])
+        interleave_vector((2, 1), 0, P)
+        interleave_scalar((2, 1), P, N)
+        quantise((2, 1))
+
+        place = {(0, 0): 0, (0, 1): HALF, (1, 1): 2 * HALF, (1, 0): 3 * HALF}
+        ez = sb([P, TILES * S], F32, "ez")
+        soft = sb([P, TILES * S], F32, "soft")
+        for c in range(2):
+            nc.vector.tensor_copy(picked[1][:, halves[c]], words[1][:].bitcast(U32).indirect(offs_t[:, list_halves[c]]))
+            for h in range(TILES):
+                product(acc_z[h, c], 2, 1, h, halves[c])
+            for h in range(TILES):
+                nc.scalar.activation(ez[:, place[h, c] : place[h, c] + HALF], acc_z[h, c][:], ACT.Exp)
+        for o in range(PASSES):
+            interleave_vector((1, o))
+        for o in range(PASSES):
+            quantise((1, o))
+            for h in range(TILES):
+                product(acc_y[h], 1, o, h, slice(0, S))
+        cut = S + 8
+        nc.scalar.activation(soft[:, :cut], ez[:, :cut], ACT.Ln, bias=1.0)
+        nc.scalar.activation(soft[:, cut:], ez[:, cut:], ACT.Ln, bias=1.0)
+
+        ang = [sb([P, S], F32, f"ang{h}") for h in range(TILES)]
+        pair = [sb([P, HALF], F32, f"pair{h}") for h in range(TILES)]
+        shared = sb([P, 3 * S], F32, "shared")
+        zeta = [shared[:, 0:S], shared[:, S + HALF : 2 * S + HALF]]
+        attr = [shared[:, S : 2 * S], shared[:, 2 * S : 3 * S]]
+        for h in range(TILES):
+            for c in range(2):
+                nc.vector.scalar_tensor_tensor(
+                    ang[h][:, halves[c]],
+                    soft[:, place[h, c] : place[h, c] + HALF],
+                    SOFTPLUS_LINEAR,
+                    acc_z[h, c][:],
+                    ALU.min,
+                    ALU.max,
+                )
+        for h in range(TILES):
+            nc.vector.tensor_tensor(pair[h][:], ang[h][:, 0::2], ang[h][:, 1::2], ALU.add)
+        for h in range(TILES):
+            mate = ang[h][:].rearrange("p (v g e) -> p v g e", g=2, e=2)[:, :, :, ::-1]
+            other = pair[h][:].rearrange("p (v g) -> p v g", g=2)[:, :, ::-1]
+            nc.vector.tensor_tensor(
+                zeta[h].rearrange("p (v g e) -> p v g e", g=2, e=2),
+                mate,
+                other.unsqueeze(3).to_broadcast([P, S // D, 2, 2]),
+                ALU.add,
+            )
+        root = [sb([P, S], F32, f"root{h}") for h in range(TILES)]
+        for h in range(TILES):
+            nc.scalar.activation(root[h][:], zeta[h], ACT.Abs_reciprocal_sqrt, scale=0.8, bias=1.0)
+        for h in range(TILES):
+            nc.scalar.activation(attr[h], acc_y[h][:], ACT.Exp, scale=-0.4)
+
+        order = [sb([P, S], F32, f"order{h}") for h in range(TILES)]
+        fetched = [sb([P, S], F32, f"fetched{h}") for h in range(TILES)]
+        both = [sb([P, S], F32, f"both{h}") for h in range(TILES)]
+        total = [sb([P, S], F32, f"total{h}") for h in range(TILES)]
+        energy = [sb([P, S], F32, f"energy{h}") for h in range(TILES)]
+
+        def fetch(h, c):
+            nc.vector.tensor_copy(fetched[h][:, halves[c]], order[h][:].indirect(rev_t[:, list_halves[c]]))
+
+        def finish(h, cols):
+            nc.vector.tensor_tensor(energy[h][:, cols], total[h][:, cols], attr[h][:, cols], ALU.mult)
+            nc.sync.dma_start(out=out[h * P : (h + 1) * P, cols], in_=energy[h][:, cols])
+
+        for h in range(TILES):
+            nc.vector.scalar_tensor_tensor(order[h][:], root[h][:], -0.5, strg_t[:], ALU.mult, ALU.mult)
+        fetch(0, 0)
+        fetch(0, 1)
+        fetch(1, 0)
+        nc.vector.tensor_tensor(both[0][:], order[0][:], fetched[0][:], ALU.add)
+        fetch(1, 1)
+        nc.vector.tensor_tensor(total[0][:], both[0][:], attr[0], ALU.add)
+        nc.vector.tensor_tensor(both[1][:], order[1][:], fetched[1][:], ALU.add)
+        finish(0, slice(0, S))
+        for cols in halves:
+            nc.vector.tensor_tensor(total[1][:, cols], both[1][:, cols], attr[1][:, cols], ALU.add)
+        for cols in halves:
+            finish(1, cols)

@@ -30,8 +30,8 @@ def tile_picked_yterso_sym_p_kernel(tc, x_words, x_scales, w1, w2, strg, offs, r
         keep = ctx.enter_context(tc.tile_pool(name="keep", bufs=1))
         psum = ctx.enter_context(tc.psum_pool(name="psum", bufs=1))
 
-        def sb(shape, dtype, name):
-            return keep.tile(shape, dtype, name=name, align_bytes=64)
+        def sb(shape, dtype, name, tag=None):
+            return keep.tile(shape, dtype, name=name, tag=tag or name, align_bytes=64)
 
         offs_t = keep.tile([P, S // 16], U16, name="offs_t")
         rev_t = keep.tile([P, S // 16], U16, name="rev_t")
@@ -50,12 +50,12 @@ def tile_picked_yterso_sym_p_kernel(tc, x_words, x_scales, w1, w2, strg, offs, r
 
         nc.vector.memset(planes[:].bitcast(I32), 0)
         nc.sync.dma_start(offs_t[:], offs)
+        load_words(0)
         for q in range(4):
             nc.sync.dma_start(
                 out=planes[32 * q : 32 * q + 4 * PASSES, :].bitcast(I32),
                 in_=x_scales[:, 4 * q : 4 * q + 4, :].bitcast(I32),
             )
-        load_words(0)
         load_weight(2, 0)
         load_weight(2, 1)
         load_words(1)
@@ -64,9 +64,9 @@ def tile_picked_yterso_sym_p_kernel(tc, x_words, x_scales, w1, w2, strg, offs, r
         nc.sync.dma_start(rev_t[:], rev)
         nc.sync.dma_start(out=strg_t[:], in_=strg)
 
-        picked = [sb([P, S], U32, f"picked{o}") for o in range(PASSES)]
+        picked = [sb([P, S], U32, "picked0")]
         picked_planes = sb([P, S], U8, "picked_planes")
-        grouped = {key: sb([P, N * PACK], BF16, f"grouped{key[0]}{key[1]}") for key in raw}
+        grouped = {(2, o): sb([P, N * PACK], BF16, f"grouped2{o}")[:] for o in range(PASSES)}
         codes = {key: sb([P, N], U32, f"codes{key[0]}{key[1]}") for key in raw}
         scales = {key: sb([P, N], U8, f"scales{key[0]}{key[1]}") for key in raw}
 
@@ -108,8 +108,8 @@ def tile_picked_yterso_sym_p_kernel(tc, x_words, x_scales, w1, w2, strg, offs, r
                 stop=(o == PASSES - 1),
             )
 
-        nc.vector.tensor_copy(picked_planes[:], planes[:].indirect(offs_t[:]))
         nc.vector.tensor_copy(picked[0][:], words[0][:].bitcast(U32).indirect(offs_t[:]))
+        nc.vector.tensor_copy(picked_planes[:], planes[:].indirect(offs_t[:]))
         interleave_scalar((2, 0))
         quantise((2, 0))
         for c in range(2):
@@ -118,6 +118,7 @@ def tile_picked_yterso_sym_p_kernel(tc, x_words, x_scales, w1, w2, strg, offs, r
         interleave_vector((2, 1), 0, P)
         interleave_scalar((2, 1), P, N)
         quantise((2, 1))
+        picked.append(sb([P, S], U32, "picked1", tag="grouped21"))
 
         place = {(0, 0): 0, (0, 1): HALF, (1, 1): 2 * HALF, (1, 0): 3 * HALF}
         ez = sb([P, TILES * S], F32, "ez")
@@ -128,7 +129,9 @@ def tile_picked_yterso_sym_p_kernel(tc, x_words, x_scales, w1, w2, strg, offs, r
                 product(acc_z[h, c], 2, 1, h, halves[c])
             for h in range(TILES):
                 nc.scalar.activation(ez[:, place[h, c] : place[h, c] + HALF], acc_z[h, c][:], ACT.Exp)
+        grouped1 = sb([P, PASSES * N * PACK], BF16, "grouped1", tag="words1")
         for o in range(PASSES):
+            grouped[1, o] = grouped1[:, o * N * PACK : (o + 1) * N * PACK]
             interleave_vector((1, o))
         for o in range(PASSES):
             quantise((1, o))
@@ -143,19 +146,21 @@ def tile_picked_yterso_sym_p_kernel(tc, x_words, x_scales, w1, w2, strg, offs, r
         shared = sb([P, 3 * S], F32, "shared")
         zeta = [shared[:, 0:S], shared[:, S + HALF : 2 * S + HALF]]
         attr = [shared[:, S : 2 * S], shared[:, 2 * S : 3 * S]]
-        for h in range(TILES):
-            for c in range(2):
-                nc.vector.scalar_tensor_tensor(
-                    ang[h][:, halves[c]],
-                    soft[:, place[h, c] : place[h, c] + HALF],
-                    SOFTPLUS_LINEAR,
-                    acc_z[h, c][:],
-                    ALU.min,
-                    ALU.max,
-                )
-        for h in range(TILES):
+
+        def guard(h, c):
+            nc.vector.scalar_tensor_tensor(
+                ang[h][:, halves[c]],
+                soft[:, place[h, c] : place[h, c] + HALF],
+                SOFTPLUS_LINEAR,
+                acc_z[h, c][:],
+                ALU.min,
+                ALU.max,
+            )
+
+        def add_pairs(h):
             nc.vector.tensor_tensor(pair[h][:], ang[h][:, 0::2], ang[h][:, 1::2], ALU.add)
-        for h in range(TILES):
+
+        def add_others(h):
             mate = ang[h][:].rearrange("p (v g e) -> p v g e", g=2, e=2)[:, :, :, ::-1]
             other = pair[h][:].rearrange("p (v g) -> p v g", g=2)[:, :, ::-1]
             nc.vector.tensor_tensor(
@@ -164,6 +169,15 @@ def tile_picked_yterso_sym_p_kernel(tc, x_words, x_scales, w1, w2, strg, offs, r
                 other.unsqueeze(3).to_broadcast([P, S // D, 2, 2]),
                 ALU.add,
             )
+
+        guard(0, 0)
+        guard(0, 1)
+        guard(1, 0)
+        add_pairs(0)
+        guard(1, 1)
+        add_others(0)
+        add_pairs(1)
+        add_others(1)
         root = [sb([P, S], F32, f"root{h}") for h in range(TILES)]
         for h in range(TILES):
             nc.scalar.activation(root[h][:], zeta[h], ACT.Abs_reciprocal_sqrt, scale=0.8, bias=1.0)

@@ -49,8 +49,8 @@ def tile_picked_yterso_sym_p_kernel(tc, x_words, x_scales, w1, w2, strg, offs, r
             nc.sync.dma_start(out=raw[w, o][:], in_=rows.rearrange("(p j) m -> p j m", j=PACK))
 
         nc.vector.memset(planes[:].bitcast(I32), 0)
-        nc.sync.dma_start(offs_t[:], offs)
         load_words(0)
+        nc.sync.dma_start(offs_t[:], offs)
         for q in range(4):
             nc.sync.dma_start(
                 out=planes[32 * q : 32 * q + 4 * PASSES, :].bitcast(I32),
@@ -120,7 +120,7 @@ def tile_picked_yterso_sym_p_kernel(tc, x_words, x_scales, w1, w2, strg, offs, r
         quantise((2, 1))
         picked.append(sb([P, S], U32, "picked1", tag="grouped21"))
 
-        place = {(0, 0): 0, (0, 1): HALF, (1, 1): 2 * HALF, (1, 0): 3 * HALF}
+        place = {(1, 1): 0, (0, 0): HALF, (0, 1): 2 * HALF, (1, 0): 3 * HALF}
         ez = sb([P, TILES * S], F32, "ez")
         soft = sb([P, TILES * S], F32, "soft")
         for c in range(2):
@@ -137,15 +137,13 @@ def tile_picked_yterso_sym_p_kernel(tc, x_words, x_scales, w1, w2, strg, offs, r
             quantise((1, o))
             for h in range(TILES):
                 product(acc_y[h], 1, o, h, slice(0, S))
-        cut = S + 8
-        nc.scalar.activation(soft[:, :cut], ez[:, :cut], ACT.Ln, bias=1.0)
-        nc.scalar.activation(soft[:, cut:], ez[:, cut:], ACT.Ln, bias=1.0)
+        cut = HALF - 8
+        for lo, hi in ((cut, 2 * HALF), (2 * HALF, 3 * HALF), (3 * HALF, 4 * HALF), (0, cut)):
+            nc.scalar.activation(soft[:, lo:hi], ez[:, lo:hi], ACT.Ln, bias=1.0)
 
         ang = [sb([P, S], F32, f"ang{h}") for h in range(TILES)]
         pair = [sb([P, HALF], F32, f"pair{h}") for h in range(TILES)]
-        shared = sb([P, 3 * S], F32, "shared")
-        zeta = [shared[:, 0:S], shared[:, S + HALF : 2 * S + HALF]]
-        attr = [shared[:, S : 2 * S], shared[:, 2 * S : 3 * S]]
+        zeta = [sb([P, S], F32, f"zeta{h}")[:] for h in range(TILES)]
 
         def guard(h, c):
             nc.vector.scalar_tensor_tensor(
@@ -181,17 +179,11 @@ def tile_picked_yterso_sym_p_kernel(tc, x_words, x_scales, w1, w2, strg, offs, r
         root = [sb([P, S], F32, f"root{h}") for h in range(TILES)]
         for h in range(TILES):
             nc.scalar.activation(root[h][:], zeta[h], ACT.Abs_reciprocal_sqrt, scale=0.8, bias=1.0)
-        for h in range(TILES):
-            nc.scalar.activation(attr[h], acc_y[h][:], ACT.Exp, scale=-0.4)
-
         order = [sb([P, S], F32, f"order{h}") for h in range(TILES)]
-        fetched = [sb([P, S], F32, f"fetched{h}") for h in range(TILES)]
+        own = [sb([P, S], F32, f"own{h}") for h in range(TILES)]
         both = [sb([P, S], F32, f"both{h}") for h in range(TILES)]
         total = [sb([P, S], F32, f"total{h}") for h in range(TILES)]
         energy = [sb([P, S], F32, f"energy{h}") for h in range(TILES)]
-
-        def fetch(h, c):
-            nc.vector.tensor_copy(fetched[h][:, halves[c]], order[h][:].indirect(rev_t[:, list_halves[c]]))
 
         def finish(h, cols):
             nc.vector.tensor_tensor(energy[h][:, cols], total[h][:, cols], attr[h][:, cols], ALU.mult)
@@ -199,15 +191,27 @@ def tile_picked_yterso_sym_p_kernel(tc, x_words, x_scales, w1, w2, strg, offs, r
 
         for h in range(TILES):
             nc.vector.scalar_tensor_tensor(order[h][:], root[h][:], -0.5, strg_t[:], ALU.mult, ALU.mult)
-        fetch(0, 0)
-        fetch(0, 1)
-        fetch(1, 0)
-        nc.vector.tensor_tensor(both[0][:], order[0][:], fetched[0][:], ALU.add)
-        fetch(1, 1)
+        nc.scalar.copy(own[0][:], order[0][:])
+        attr = [sb([P, S], F32, f"attr{h}", tag=f"root{h}")[:] for h in range(TILES)]
+        for h in range(TILES):
+            nc.scalar.activation(attr[h], acc_y[h][:], ACT.Exp, scale=-0.4)
+
+        def fetch_and_add(h, c):
+            nc.vector.tensor_tensor(
+                both[h][:, halves[c]],
+                order[h][:].indirect(rev_t[:, list_halves[c]]),
+                own[h][:, halves[c]],
+                ALU.add,
+            )
+
+        fetch_and_add(0, 0)
+        nc.vector.tensor_copy(own[1][:], order[1][:])
+        fetch_and_add(0, 1)
+        fetch_and_add(1, 0)
+        fetch_and_add(1, 1)
         nc.vector.tensor_tensor(total[0][:], both[0][:], attr[0], ALU.add)
-        nc.vector.tensor_tensor(both[1][:], order[1][:], fetched[1][:], ALU.add)
+        nc.vector.tensor_tensor(total[1][:, halves[0]], both[1][:, halves[0]], attr[1][:, halves[0]], ALU.add)
         finish(0, slice(0, S))
-        for cols in halves:
-            nc.vector.tensor_tensor(total[1][:, cols], both[1][:, cols], attr[1][:, cols], ALU.add)
+        nc.vector.tensor_tensor(total[1][:, halves[1]], both[1][:, halves[1]], attr[1][:, halves[1]], ALU.add)
         for cols in halves:
             finish(1, cols)

@@ -20,7 +20,12 @@ PACK = 4
 K_PASS = P * PACK
 PASSES = K // K_PASS
 TILES = N // P
+QUADRANT = 32
+SCALE_ROWS = 4
+LIST_ROWS = 16
 HALF = S // 2
+RUN = 4
+LN_OVERLAP = 8
 SOFTPLUS_LINEAR = 40.0
 
 
@@ -33,10 +38,10 @@ def tile_picked_yterso_sym_p_kernel(tc, x_words, x_scales, w1, w2, strg, offs, r
         def sb(shape, dtype, name, tag=None):
             return keep.tile(shape, dtype, name=name, tag=tag or name, align_bytes=64)
 
-        offs_t = keep.tile([P, S // 16], U16, name="offs_t")
-        rev_t = keep.tile([P, S // 16], U16, name="rev_t")
+        offs_t = keep.tile([P, S // LIST_ROWS], U16, name="offs_t")
+        rev_t = keep.tile([P, S // LIST_ROWS], U16, name="rev_t")
         words = [sb([P, T], I32, f"words{o}") for o in range(PASSES)]
-        planes = sb([P, T], U8, "planes")
+        x_scale_t = sb([P, T], U8, "x_scale_t")
         raw = {(w, o): sb([P, PACK, N], F32, f"raw{w}{o}") for w in (1, 2) for o in range(PASSES)}
         strg_t = sb([P, S], F32, "strg_t")
         weights = {1: w1, 2: w2}
@@ -46,15 +51,15 @@ def tile_picked_yterso_sym_p_kernel(tc, x_words, x_scales, w1, w2, strg, offs, r
 
         def load_weight(w, o):
             rows = weights[w][o * K_PASS : (o + 1) * K_PASS, :]
-            nc.sync.dma_start(out=raw[w, o][:], in_=rows.rearrange("(p j) m -> p j m", j=PACK))
+            nc.sync.dma_start(out=raw[w, o][:], in_=rows.rearrange("(p t) m -> p t m", t=PACK))
 
-        nc.vector.memset(planes[:].bitcast(I32), 0)
+        nc.vector.memset(x_scale_t[:].bitcast(I32), 0)
         load_words(0)
         nc.sync.dma_start(offs_t[:], offs)
-        for q in range(4):
+        for q in range(P // QUADRANT):
             nc.sync.dma_start(
-                out=planes[32 * q : 32 * q + 4 * PASSES, :].bitcast(I32),
-                in_=x_scales[:, 4 * q : 4 * q + 4, :].bitcast(I32),
+                out=x_scale_t[QUADRANT * q : QUADRANT * q + SCALE_ROWS * PASSES, :].bitcast(I32),
+                in_=x_scales[:, SCALE_ROWS * q : SCALE_ROWS * (q + 1), :].bitcast(I32),
             )
         load_weight(2, 0)
         load_weight(2, 1)
@@ -65,33 +70,29 @@ def tile_picked_yterso_sym_p_kernel(tc, x_words, x_scales, w1, w2, strg, offs, r
         nc.sync.dma_start(out=strg_t[:], in_=strg)
 
         picked = [sb([P, S], U32, "picked0")]
-        picked_planes = sb([P, S], U8, "picked_planes")
+        picked_scale = sb([P, S], U8, "picked_scale")
         grouped = {(2, o): sb([P, N * PACK], BF16, f"grouped2{o}")[:] for o in range(PASSES)}
         codes = {key: sb([P, N], U32, f"codes{key[0]}{key[1]}") for key in raw}
-        scales = {key: sb([P, N], U8, f"scales{key[0]}{key[1]}") for key in raw}
+        w_scale = {key: sb([P, N], U8, f"w_scale{key[0]}{key[1]}") for key in raw}
 
         halves = [slice(c * HALF, (c + 1) * HALF) for c in range(2)]
-        list_halves = [slice(c * HALF // 16, (c + 1) * HALF // 16) for c in range(2)]
+        list_halves = [slice(c * HALF // LIST_ROWS, (c + 1) * HALF // LIST_ROWS) for c in range(2)]
 
-        def views(key, lo, hi):
-            dst = grouped[key][:, lo * PACK : hi * PACK].rearrange("p (c i t) -> p c t i", i=4, t=PACK)
-            src = raw[key][:, :, lo:hi].rearrange("p t (c i) -> p c t i", i=4)
+        def interleave_views(key, lo, hi):
+            dst = grouped[key][:, lo * PACK : hi * PACK].rearrange("p (c i t) -> p c t i", i=RUN, t=PACK)
+            src = raw[key][:, :, lo:hi].rearrange("p t (c i) -> p c t i", i=RUN)
             return dst, src
 
         def interleave_scalar(key, lo=0, hi=N):
-            dst, src = views(key, lo, hi)
+            dst, src = interleave_views(key, lo, hi)
             nc.scalar.activation(dst, src, ACT.Copy)
 
         def interleave_vector(key, lo=0, hi=N):
-            dst, src = views(key, lo, hi)
+            dst, src = interleave_views(key, lo, hi)
             nc.vector.tensor_copy(dst, src)
 
-        def quantise(key, lo=0, hi=N):
-            nc.vector.quantize_mx(
-                out=codes[key][:, lo:hi].bitcast(FP8X4),
-                scales=scales[key][:, lo:hi],
-                in_=grouped[key][:, lo * PACK : hi * PACK],
-            )
+        def quantise(key):
+            nc.vector.quantize_mx(out=codes[key][:].bitcast(FP8X4), scales=w_scale[key][:], in_=grouped[key])
 
         acc_z = {(h, c): psum.tile([P, HALF], F32, name=f"acc_z{h}{c}") for h in range(TILES) for c in range(2)}
         acc_y = [psum.tile([P, S], F32, name=f"acc_y{h}") for h in range(TILES)]
@@ -101,34 +102,36 @@ def tile_picked_yterso_sym_p_kernel(tc, x_words, x_scales, w1, w2, strg, offs, r
             nc.tensor.matmul_mx(
                 out=acc[:],
                 lhsT=codes[w, o][:, rows].bitcast(FP8X4),
-                lhsT_scale=scales[w, o][:, rows],
+                lhsT_scale=w_scale[w, o][:, rows],
                 rhs=picked[o][:, cols].bitcast(FP8X4),
-                rhs_scale=picked_planes[4 * o : P, cols],
+                rhs_scale=picked_scale[SCALE_ROWS * o : P, cols],
                 start=(o == 0),
                 stop=(o == PASSES - 1),
             )
 
         nc.vector.tensor_copy(picked[0][:], words[0][:].bitcast(U32).indirect(offs_t[:]))
-        nc.vector.tensor_copy(picked_planes[:], planes[:].indirect(offs_t[:]))
+        nc.vector.tensor_copy(picked_scale[:], x_scale_t[:].indirect(offs_t[:]))
         interleave_scalar((2, 0))
         quantise((2, 0))
         for c in range(2):
             for h in range(TILES):
                 product(acc_z[h, c], 2, 0, h, halves[c])
+
         interleave_vector((2, 1), 0, P)
         interleave_scalar((2, 1), P, N)
         quantise((2, 1))
         picked.append(sb([P, S], U32, "picked1", tag="grouped21"))
 
         place = {(1, 1): 0, (0, 0): HALF, (0, 1): 2 * HALF, (1, 0): 3 * HALF}
-        ez = sb([P, TILES * S], F32, "ez")
+        exp_z = sb([P, TILES * S], F32, "exp_z")
         soft = sb([P, TILES * S], F32, "soft")
         for c in range(2):
             nc.vector.tensor_copy(picked[1][:, halves[c]], words[1][:].bitcast(U32).indirect(offs_t[:, list_halves[c]]))
             for h in range(TILES):
                 product(acc_z[h, c], 2, 1, h, halves[c])
             for h in range(TILES):
-                nc.scalar.activation(ez[:, place[h, c] : place[h, c] + HALF], acc_z[h, c][:], ACT.Exp)
+                nc.scalar.activation(exp_z[:, place[h, c] : place[h, c] + HALF], acc_z[h, c][:], ACT.Exp)
+
         grouped1 = sb([P, PASSES * N * PACK], BF16, "grouped1", tag="words1")
         for o in range(PASSES):
             grouped[1, o] = grouped1[:, o * N * PACK : (o + 1) * N * PACK]
@@ -137,64 +140,55 @@ def tile_picked_yterso_sym_p_kernel(tc, x_words, x_scales, w1, w2, strg, offs, r
             quantise((1, o))
             for h in range(TILES):
                 product(acc_y[h], 1, o, h, slice(0, S))
-        cut = HALF - 8
+
+        cut = HALF - LN_OVERLAP
         for lo, hi in ((cut, 2 * HALF), (2 * HALF, 3 * HALF), (3 * HALF, 4 * HALF), (0, cut)):
-            nc.scalar.activation(soft[:, lo:hi], ez[:, lo:hi], ACT.Ln, bias=1.0)
+            nc.scalar.activation(soft[:, lo:hi], exp_z[:, lo:hi], ACT.Ln, bias=1.0)
 
         ang = [sb([P, S], F32, f"ang{h}") for h in range(TILES)]
         pair = [sb([P, HALF], F32, f"pair{h}") for h in range(TILES)]
-        zeta = [sb([P, S], F32, f"zeta{h}")[:] for h in range(TILES)]
+        zeta = [sb([P, S], F32, f"zeta{h}") for h in range(TILES)]
 
-        def guard(h, c):
-            nc.vector.scalar_tensor_tensor(
-                ang[h][:, halves[c]],
-                soft[:, place[h, c] : place[h, c] + HALF],
-                SOFTPLUS_LINEAR,
-                acc_z[h, c][:],
-                ALU.min,
-                ALU.max,
-            )
+        for h in range(TILES):
+            for c in range(2):
+                nc.vector.scalar_tensor_tensor(
+                    ang[h][:, halves[c]],
+                    soft[:, place[h, c] : place[h, c] + HALF],
+                    SOFTPLUS_LINEAR,
+                    acc_z[h, c][:],
+                    ALU.min,
+                    ALU.max,
+                )
 
-        def add_pairs(h):
+        for h in range(TILES):
             nc.vector.tensor_tensor(pair[h][:], ang[h][:, 0::2], ang[h][:, 1::2], ALU.add)
-
-        def add_others(h):
+        for h in range(TILES):
             mate = ang[h][:].rearrange("p (v g e) -> p v g e", g=2, e=2)[:, :, :, ::-1]
             other = pair[h][:].rearrange("p (v g) -> p v g", g=2)[:, :, ::-1]
             nc.vector.tensor_tensor(
-                zeta[h].rearrange("p (v g e) -> p v g e", g=2, e=2),
+                zeta[h][:].rearrange("p (v g e) -> p v g e", g=2, e=2),
                 mate,
                 other.unsqueeze(3).to_broadcast([P, S // D, 2, 2]),
                 ALU.add,
             )
 
-        guard(0, 0)
-        guard(0, 1)
-        guard(1, 0)
-        add_pairs(0)
-        guard(1, 1)
-        add_others(0)
-        add_pairs(1)
-        add_others(1)
         root = [sb([P, S], F32, f"root{h}") for h in range(TILES)]
         for h in range(TILES):
-            nc.scalar.activation(root[h][:], zeta[h], ACT.Abs_reciprocal_sqrt, scale=0.8, bias=1.0)
+            nc.scalar.activation(root[h][:], zeta[h][:], ACT.Abs_reciprocal_sqrt, scale=0.8, bias=1.0)
+
         order = [sb([P, S], F32, f"order{h}") for h in range(TILES)]
         own = [sb([P, S], F32, f"own{h}") for h in range(TILES)]
         both = [sb([P, S], F32, f"both{h}") for h in range(TILES)]
         total = [sb([P, S], F32, f"total{h}") for h in range(TILES)]
         energy = [sb([P, S], F32, f"energy{h}") for h in range(TILES)]
 
-        def finish(h, cols):
-            nc.vector.tensor_tensor(energy[h][:, cols], total[h][:, cols], attr[h][:, cols], ALU.mult)
-            nc.sync.dma_start(out=out[h * P : (h + 1) * P, cols], in_=energy[h][:, cols])
-
         for h in range(TILES):
             nc.vector.scalar_tensor_tensor(order[h][:], root[h][:], -0.5, strg_t[:], ALU.mult, ALU.mult)
         nc.scalar.copy(own[0][:], order[0][:])
-        attr = [sb([P, S], F32, f"attr{h}", tag=f"root{h}")[:] for h in range(TILES)]
+
+        attr = [sb([P, S], F32, f"attr{h}", tag=f"root{h}") for h in range(TILES)]
         for h in range(TILES):
-            nc.scalar.activation(attr[h], acc_y[h][:], ACT.Exp, scale=-0.4)
+            nc.scalar.activation(attr[h][:], acc_y[h][:], ACT.Exp, scale=-0.4)
 
         def fetch_and_add(h, c):
             nc.vector.tensor_tensor(
@@ -204,14 +198,21 @@ def tile_picked_yterso_sym_p_kernel(tc, x_words, x_scales, w1, w2, strg, offs, r
                 ALU.add,
             )
 
+        def add_attr(h, cols):
+            nc.vector.tensor_tensor(total[h][:, cols], both[h][:, cols], attr[h][:, cols], ALU.add)
+
+        def finish(h, cols):
+            nc.vector.tensor_tensor(energy[h][:, cols], total[h][:, cols], attr[h][:, cols], ALU.mult)
+            nc.sync.dma_start(out=out[h * P : (h + 1) * P, cols], in_=energy[h][:, cols])
+
         fetch_and_add(0, 0)
         nc.vector.tensor_copy(own[1][:], order[1][:])
         fetch_and_add(0, 1)
         fetch_and_add(1, 0)
         fetch_and_add(1, 1)
-        nc.vector.tensor_tensor(total[0][:], both[0][:], attr[0], ALU.add)
-        nc.vector.tensor_tensor(total[1][:, halves[0]], both[1][:, halves[0]], attr[1][:, halves[0]], ALU.add)
+        add_attr(0, slice(0, S))
+        add_attr(1, halves[0])
         finish(0, slice(0, S))
-        nc.vector.tensor_tensor(total[1][:, halves[1]], both[1][:, halves[1]], attr[1][:, halves[1]], ALU.add)
+        add_attr(1, halves[1])
         for cols in halves:
             finish(1, cols)

from contextlib import ExitStack

import concourse.mybir as mybir

K, T, S, D, N = 1024, 1024, 512, 4, 256
FLOPS = 2 * 2 * K * N * S

F32 = mybir.dt.float32
BF16 = mybir.dt.bfloat16
I32 = mybir.dt.int32
U32 = mybir.dt.uint32
U16 = mybir.dt.uint16
U8 = mybir.dt.uint8
FP8X4 = mybir.dt.float8_e4m3fn_x4
ALU = mybir.AluOpType
ACT = mybir.ActivationFunctionType

P = 128
PACK = 4
K_PASS = P * PACK
PASSES = K // K_PASS
TILES = N // P
QUADRANT = 32
SCALE_ROWS = 4
LIST_ROWS = 16
HALF = S // 2
RUN = 4
LN_OVERLAP = 8
SOFTPLUS_LINEAR = 40.0


def tile_picked_yterso_sym_p_kernel(tc, x_words, x_scales, w1, w2, strg, offs, rev, out):
    nc = tc.nc
    with ExitStack() as ctx:
        keep = ctx.enter_context(tc.tile_pool(name="keep", bufs=1))
        psum = ctx.enter_context(tc.psum_pool(name="psum", bufs=1))

        def sb(shape, dtype, name, tag=None):
            return keep.tile(shape, dtype, name=name, tag=tag or name, align_bytes=64)

        offs_t = keep.tile([P, S // LIST_ROWS], U16, name="offs_t")
        rev_t = keep.tile([P, S // LIST_ROWS], U16, name="rev_t")
        words = [sb([P, T], I32, f"words{o}") for o in range(PASSES)]
        x_scale_t = sb([P, T], U8, "x_scale_t")
        raw = {(w, o): sb([P, PACK, N], F32, f"raw{w}{o}") for w in (1, 2) for o in range(PASSES)}
        strg_t = sb([P, S], F32, "strg_t")
        weights = {1: w1, 2: w2}

        def load_words(o):
            nc.sync.dma_start(out=words[o][:], in_=x_words[o].rearrange("p n t -> p (n t)").bitcast(I32))

        def load_weight(w, o):
            rows = weights[w][o * K_PASS : (o + 1) * K_PASS, :]
            nc.sync.dma_start(out=raw[w, o][:], in_=rows.rearrange("(p t) m -> p t m", t=PACK))

        nc.vector.memset(x_scale_t[:].bitcast(I32), 0)
        load_words(0)
        nc.sync.dma_start(offs_t[:], offs)
        for q in range(P // QUADRANT):
            nc.sync.dma_start(
                out=x_scale_t[QUADRANT * q : QUADRANT * q + SCALE_ROWS * PASSES, :].bitcast(I32),
                in_=x_scales[:, SCALE_ROWS * q : SCALE_ROWS * (q + 1), :].bitcast(I32),
            )
        load_weight(2, 0)
        load_weight(2, 1)
        load_words(1)
        load_weight(1, 0)
        load_weight(1, 1)
        nc.sync.dma_start(rev_t[:], rev)
        nc.sync.dma_start(out=strg_t[:], in_=strg)

        picked = [sb([P, S], U32, "picked0")]
        picked_scale = sb([P, S], U8, "picked_scale")
        grouped = {(2, o): sb([P, N * PACK], BF16, f"grouped2{o}")[:] for o in range(PASSES)}
        codes = {key: sb([P, N], U32, f"codes{key[0]}{key[1]}") for key in raw}
        w_scale = {key: sb([P, N], U8, f"w_scale{key[0]}{key[1]}") for key in raw}

        halves = [slice(c * HALF, (c + 1) * HALF) for c in range(2)]
        list_halves = [slice(c * HALF // LIST_ROWS, (c + 1) * HALF // LIST_ROWS) for c in range(2)]

        def interleave_views(key, lo, hi):
            dst = grouped[key][:, lo * PACK : hi * PACK].rearrange("p (c i t) -> p c t i", i=RUN, t=PACK)
            src = raw[key][:, :, lo:hi].rearrange("p t (c i) -> p c t i", i=RUN)
            return dst, src

        def interleave_scalar(key, lo=0, hi=N):
            dst, src = interleave_views(key, lo, hi)
            nc.scalar.activation(dst, src, ACT.Copy)

        def interleave_vector(key, lo=0, hi=N):
            dst, src = interleave_views(key, lo, hi)
            nc.vector.tensor_copy(dst, src)

        def quantise(key):
            nc.vector.quantize_mx(out=codes[key][:].bitcast(FP8X4), scales=w_scale[key][:], in_=grouped[key])

        acc_z = {(h, c): psum.tile([P, HALF], F32, name=f"acc_z{h}{c}") for h in range(TILES) for c in range(2)}
        acc_y = [psum.tile([P, S], F32, name=f"acc_y{h}") for h in range(TILES)]

        def product(acc, w, o, h, cols):
            rows = slice(h * P, (h + 1) * P)
            nc.tensor.matmul_mx(
                out=acc[:],
                lhsT=codes[w, o][:, rows].bitcast(FP8X4),
                lhsT_scale=w_scale[w, o][:, rows],
                rhs=picked[o][:, cols].bitcast(FP8X4),
                rhs_scale=picked_scale[SCALE_ROWS * o : P, cols],
                start=(o == 0),
                stop=(o == PASSES - 1),
            )

        nc.vector.tensor_copy(picked[0][:], words[0][:].bitcast(U32).indirect(offs_t[:]))
        nc.vector.tensor_copy(picked_scale[:], x_scale_t[:].indirect(offs_t[:]))
        interleave_scalar((2, 0))
        quantise((2, 0))
        for c in range(2):
            for h in range(TILES):
                product(acc_z[h, c], 2, 0, h, halves[c])

        interleave_vector((2, 1), 0, P)
        interleave_scalar((2, 1), P, N)
        quantise((2, 1))
        picked.append(sb([P, S], U32, "picked1", tag="grouped21"))

        place = {(1, 1): 0, (0, 0): HALF, (0, 1): 2 * HALF, (1, 0): 3 * HALF}
        exp_z = sb([P, TILES * S], F32, "exp_z")
        soft = sb([P, TILES * S], F32, "soft")
        for c in range(2):
            nc.vector.tensor_copy(picked[1][:, halves[c]], words[1][:].bitcast(U32).indirect(offs_t[:, list_halves[c]]))
            for h in range(TILES):
                product(acc_z[h, c], 2, 1, h, halves[c])
            for h in range(TILES):
                nc.scalar.activation(exp_z[:, place[h, c] : place[h, c] + HALF], acc_z[h, c][:], ACT.Exp)

        grouped1 = sb([P, PASSES * N * PACK], BF16, "grouped1", tag="words1")
        for o in range(PASSES):
            grouped[1, o] = grouped1[:, o * N * PACK : (o + 1) * N * PACK]
            interleave_vector((1, o))
        for o in range(PASSES):
            quantise((1, o))
            for h in range(TILES):
                product(acc_y[h], 1, o, h, slice(0, S))

        cut = HALF - LN_OVERLAP
        for lo, hi in ((cut, 2 * HALF), (2 * HALF, 3 * HALF), (3 * HALF, 4 * HALF), (0, cut)):
            nc.scalar.activation(soft[:, lo:hi], exp_z[:, lo:hi], ACT.Ln, bias=1.0)

        ang = [sb([P, S], F32, f"ang{h}") for h in range(TILES)]
        pair = [sb([P, HALF], F32, f"pair{h}") for h in range(TILES)]
        zeta = [sb([P, S], F32, f"zeta{h}") for h in range(TILES)]

        for h in range(TILES):
            for c in range(2):
                nc.vector.scalar_tensor_tensor(
                    ang[h][:, halves[c]],
                    soft[:, place[h, c] : place[h, c] + HALF],
                    SOFTPLUS_LINEAR,
                    acc_z[h, c][:],
                    ALU.min,
                    ALU.max,
                )

        for h in range(TILES):
            nc.vector.tensor_tensor(pair[h][:], ang[h][:, 0::2], ang[h][:, 1::2], ALU.add)
        for h in range(TILES):
            mate = ang[h][:].rearrange("p (v g e) -> p v g e", g=2, e=2)[:, :, :, ::-1]
            other = pair[h][:].rearrange("p (v g) -> p v g", g=2)[:, :, ::-1]
            nc.vector.tensor_tensor(
                zeta[h][:].rearrange("p (v g e) -> p v g e", g=2, e=2),
                mate,
                other.unsqueeze(3).to_broadcast([P, S // D, 2, 2]),
                ALU.add,
            )

        root = [sb([P, S], F32, f"root{h}") for h in range(TILES)]
        for h in range(TILES):
            nc.scalar.activation(root[h][:], zeta[h][:], ACT.Abs_reciprocal_sqrt, scale=0.8, bias=1.0)

        order = [sb([P, S], F32, f"order{h}") for h in range(TILES)]
        own = [sb([P, S], F32, f"own{h}") for h in range(TILES)]
        both = [sb([P, S], F32, f"both{h}") for h in range(TILES)]
        total = [sb([P, S], F32, f"total{h}") for h in range(TILES)]
        energy = [sb([P, S], F32, f"energy{h}") for h in range(TILES)]

        for h in range(TILES):
            nc.vector.scalar_tensor_tensor(order[h][:], root[h][:], -0.5, strg_t[:], ALU.mult, ALU.mult)
        nc.scalar.copy(own[0][:], order[0][:])

        attr = [sb([P, S], F32, f"attr{h}", tag=f"root{h}") for h in range(TILES)]
        for h in range(TILES):
            nc.scalar.activation(attr[h][:], acc_y[h][:], ACT.Exp, scale=-0.4)

        def fetch_and_add(h, c):
            nc.vector.tensor_tensor(
                both[h][:, halves[c]],
                order[h][:].indirect(rev_t[:, list_halves[c]]),
                own[h][:, halves[c]],
                ALU.add,
            )

        def add_attr(h, cols):
            nc.vector.tensor_tensor(total[h][:, cols], both[h][:, cols], attr[h][:, cols], ALU.add)

        def finish(h, cols):
            nc.vector.tensor_tensor(energy[h][:, cols], total[h][:, cols], attr[h][:, cols], ALU.mult)
            nc.sync.dma_start(out=out[h * P : (h + 1) * P, cols], in_=energy[h][:, cols])

        fetch_and_add(0, 0)
        nc.vector.tensor_copy(own[1][:], order[1][:])
        fetch_and_add(0, 1)
        fetch_and_add(1, 0)
        fetch_and_add(1, 1)
        add_attr(0, slice(0, S))
        add_attr(1, halves[0])
        finish(0, slice(0, S))
        add_attr(1, halves[1])
        for cols in halves:
            finish(1, cols)
